import numpy as np
import ml_dtypes


def mxq(x, axis, fmt="e4m3"):
    dtype, down = {"e4m3": (ml_dtypes.float8_e4m3fn, 7), "e5m2": (ml_dtypes.float8_e5m2, 14)}[fmt]
    v = np.moveaxis(np.asarray(x, np.float32).astype(ml_dtypes.bfloat16).astype(np.float64), axis, -1)
    blocks = v.reshape(v.shape[:-1] + (-1, 32))
    amax = np.abs(blocks).max(-1, keepdims=True)
    byte = np.maximum(np.where(amax > 0, np.frexp(amax)[1] - 1 + 127, 0) - down, 1)
    scale = np.exp2(byte - 127.0)
    codes = (blocks / scale).astype(np.float32).astype(dtype).astype(np.float64)
    return np.moveaxis((codes * scale).reshape(v.shape), -1, axis)


WIDE = False


def mx_kscale(k):
    if not WIDE:
        return np.ones(k)
    levels = np.array([10, -10, 5, -5, 0])
    if k % 512:
        return np.exp2(np.random.permutation(np.resize(levels, k // 32))).repeat(32)
    a = np.empty((k // 512, 16))
    for p in range(k // 512):
        a[p, :8] = np.random.permutation(np.resize(levels, 8))
        for g in range(8):
            far = levels[np.abs(levels - a[p, g]) >= 10]
            a[p, g + 8] = far[np.random.randint(len(far))]
    return np.exp2(a.ravel()).repeat(32)


def f64(x):
    return np.asarray(x).astype(np.float64)


def striped(idx):
    return np.tile(idx.reshape(-1, 16).T, (8, 1)).astype(np.uint16)


def unstriped(offs):
    return offs[:16].T.reshape(-1).astype(np.int64)


def pack_weight(w):
    k, n = w.shape
    w = f64(np.asarray(w, np.float32).astype(ml_dtypes.bfloat16)).reshape(k // 32, 32, n)
    amax = np.abs(w).max(1)
    byte = np.clip(np.where(amax > 0, np.frexp(amax)[1] - 1 + 127 - 7, 1), 1, 254)
    scaled = (w * np.exp2(127.0 - byte)[:, None, :]).reshape(k, n).astype(np.float32)
    words = np.ascontiguousarray(scaled.reshape(k // 512, 128, 4, n).transpose(0, 1, 3, 2)).astype(ml_dtypes.float8_e4m3fn).view(np.uint8)
    return words, np.ascontiguousarray(byte.astype(np.uint8).reshape(k // 512, 16, n))


def unpack_weight(words, scales):
    g, p, n, _ = words.shape
    vals = np.ascontiguousarray(words).view(ml_dtypes.float8_e4m3fn).astype(np.float64) * np.repeat(np.exp2(scales.astype(np.float64) - 127.0), 8, axis=1)[..., None]
    return vals.transpose(0, 1, 3, 2).reshape(g * 512, n)


def sigmoid(v):
    return 1.0 / (1.0 + np.exp(-np.maximum(v, -700.0)))


K, T, S, N, D = 512, 2048, 512, 256, 3
P = 2 ** 7


def setup_inputs():
    n = np.random.standard_normal
    s = mx_kscale(K)[:, None]
    packed_xT = pack_weight(n((K, T)) * s)
    return {
        "x_words": packed_xT[0],
        "x_scales": packed_xT[1],
        "w1": (n((K, N)) / np.sqrt(K) / s).astype(np.float32),
        "adopt": (np.random.uniform(0.0, 0.7, (N, S))).astype(np.float32),
        "infl": (np.tile(np.random.uniform(0.1, 0.6, (D, 1, S)), (1, P, 1))).astype(np.float32),
        "offs": striped(np.random.permutation(T)[:S]),
        "pos1": striped(np.random.permutation(S)[:S]),
        "pos2": striped(np.random.permutation(S)[:S]),
        "pos3": striped(np.random.permutation(S)[:S]),
    }


def reference(x_words, x_scales, w1, adopt, infl, offs, pos1, pos2, pos3):
    xq = unpack_weight(x_words, x_scales)[:, unstriped(offs)]
    y = mxq(f64(w1), 0, "e4m3").T @ xq
    inn = 0.4 * sigmoid(y)
    hza = -1.0 * ((-1.0 * inn + 1.0) * (np.exp(-1.0 * (f64(adopt)[:, unstriped(pos1)] * f64(infl)[0, :1] + f64(adopt)[:, unstriped(pos2)] * f64(infl)[1, :1] + f64(adopt)[:, unstriped(pos3)] * f64(infl)[2, :1])))) + 1.0
    ada = f64(adopt) + (-1.0 * f64(adopt) + 1.0) * hza
    hzb = -1.0 * ((-1.0 * inn + 1.0) * (np.exp(-1.0 * (ada[:, unstriped(pos1)] * f64(infl)[0, :1] + ada[:, unstriped(pos2)] * f64(infl)[1, :1] + ada[:, unstriped(pos3)] * f64(infl)[2, :1])))) + 1.0
    return ada + (-1.0 * ada + 1.0) * hzb

@@ -1,0 +1,130 @@
+from contextlib import ExitStack
+
+import concourse.mybir as mybir
+from concourse.masks import make_identity
+
+F32 = mybir.dt.float32
+BF16 = mybir.dt.bfloat16
+I32 = mybir.dt.int32
+U32 = mybir.dt.uint32
+U16 = mybir.dt.uint16
+U8 = mybir.dt.uint8
+FP8X4 = mybir.dt.float8_e4m3fn_x4
+ACT = mybir.ActivationFunctionType
+ALU = mybir.AluOpType
+
+K, T, S, N, D = 512, 2048, 512, 256, 3
+P = 128
+BLOCKS = N // P
+CHUNKS = S // P
+SPARE = 16
+FLOPS = 2 * K * N * S
+
+
+def tile_picked_ybassn_two_p_kernel(tc, x_words, x_scales, w1, adopt, infl, offs, pos1, pos2, pos3, out):
+    nc = tc.nc
+    with ExitStack() as ctx:
+        keep = ctx.enter_context(tc.tile_pool(name="keep", bufs=1))
+        psum = ctx.enter_context(tc.psum_pool(name="psum", bufs=1))
+
+        pos_dram = (pos1, pos2, pos3)
+        pos = [keep.tile([P, S // 16], U16, name=f"pos{d}") for d in range(D)]
+        picks = keep.tile([P, S // 16], U16, name="picks")
+        before = [keep.tile([P, S + SPARE], F32, name=f"before{b}") for b in range(BLOCKS)]
+        left = [keep.tile([P, S + SPARE], F32, name=f"left{b}") for b in range(BLOCKS)]
+        weight = [keep.tile([P, S], F32, name=f"weight{d}") for d in range(D)]
+        w_raw = keep.tile([P, 4, N], F32, name="w_raw")
+        words = keep.tile([P, T], I32, name="words")
+        bytes_in = keep.tile([P, T], U8, name="bytes_in")
+        ident = keep.tile([P, P], F32, name="ident")
+
+        make_identity(nc, ident[:])
+        for b in range(BLOCKS):
+            nc.vector.memset(before[b][:, S:], 0.0)
+            nc.vector.memset(left[b][:, S:], 0.0)
+        nc.vector.memset(bytes_in[:].bitcast(I32), 0)
+        for q in range(4):
+            nc.gpsimd.dma_start(bytes_in[32 * q : 32 * q + 4, :].bitcast(I32), x_scales[0, 4 * q : 4 * q + 4, :].bitcast(I32))
+
+        nc.sync.dma_start(pos[0][:], pos_dram[0])
+        nc.sync.dma_start(before[0][:, :S], adopt[0:P, :])
+        nc.sync.dma_start(weight[0][:], infl[0])
+        for d in range(1, D):
+            nc.sync.dma_start(pos[d][:], pos_dram[d])
+            nc.sync.dma_start(weight[d][:], infl[d])
+        nc.sync.dma_start(w_raw[:], w1.rearrange("(p j) n -> p j n", j=4))
+        nc.sync.dma_start(picks[:], offs)
+        nc.sync.dma_start(words[:], x_words[0].rearrange("p n t -> p (n t)").bitcast(I32))
+        nc.sync.dma_start(before[1][:, :S], adopt[P : 2 * P, :])
+
+        def add_turned(bank, src, first, last):
+            for c in range(CHUNKS):
+                cols = slice(c * P, (c + 1) * P)
+                nc.tensor.matmul(bank[:, cols], src[:, cols], ident[:], start=first and c == 0, stop=last and c == CHUNKS - 1, is_transpose=True)
+
+        def pressure(window, bank, opened, tag):
+            for d in range(D):
+                term = keep.tile([P, S], F32, name=f"term{tag}{d}")
+                nc.vector.tensor_tensor(term[:], window[:].indirect(pos[d][:]), weight[d][:], ALU.mult)
+                add_turned(bank, term, first=(d == 0 and not opened), last=(d == D - 1))
+
+        def decay(bank, tag, bank_tag):
+            turned = keep.tile([P, S], F32, name=f"turned{tag}")
+            nc.scalar.activation(turned[:], bank[:], ACT.Exp, scale=-1.0)
+            back = psum.tile([P, S], F32, name=f"back{tag}", tag=bank_tag)
+            for c in range(CHUNKS):
+                cols = slice(c * P, (c + 1) * P)
+                nc.tensor.transpose(back[:, cols], turned[:, cols], ident[:])
+            return back
+
+        first_sum = [psum.tile([P, S], F32, name=f"first_sum{b}", tag=f"first{b}") for b in range(BLOCKS)]
+        second_sum = [psum.tile([P, S], F32, name=f"second_sum{b}", tag=f"second{b}") for b in range(BLOCKS)]
+
+        not_yet = [keep.tile([P, S], F32, name=f"not_yet{b}") for b in range(BLOCKS)]
+        nc.scalar.activation(not_yet[0][:], before[0][:, :S], ACT.Copy, scale=-0.2, bias=0.2)
+
+        pressure(before[0], first_sum[0], False, "a0")
+        first_decay = [decay(first_sum[0], "a0", "back0")]
+
+        w_grouped = keep.tile([P, N, 4], BF16, name="w_grouped", align_bytes=64)
+        nc.scalar.copy(w_grouped[:], w_raw[:].rearrange("p j n -> p n j"))
+        w_codes = keep.tile([P, N], U32, name="w_codes", align_bytes=64)
+        w_scales = keep.tile([P, N], U8, name="w_scales", align_bytes=64)
+        nc.vector.quantize_mx(w_codes[:].bitcast(FP8X4), w_scales[:], w_grouped[:].rearrange("p n j -> p (n j)"))
+        x_codes = keep.tile([P, S], U32, name="x_codes", align_bytes=64)
+        x_bytes = keep.tile([P, S], U8, name="x_bytes", align_bytes=64)
+        nc.vector.tensor_copy(x_bytes[:], bytes_in[:].indirect(picks[:]))
+        nc.vector.tensor_copy(x_codes[:], words[:].bitcast(U32).indirect(picks[:]))
+        half = []
+        for b in range(BLOCKS):
+            cols = slice(b * P, (b + 1) * P)
+            y = psum.tile([P, S], F32, name=f"y{b}", tag=f"y{b}")
+            nc.tensor.matmul_mx(out=y[:], lhsT=w_codes[:, cols].bitcast(FP8X4), lhsT_scale=w_scales[:, cols],
+                                rhs=x_codes[:].bitcast(FP8X4), rhs_scale=x_bytes[:], start=True, stop=True)
+            t = keep.tile([P, S], F32, name=f"half{b}")
+            nc.scalar.activation(t[:], y[:], ACT.Tanh, scale=0.5)
+            half.append(t)
+        nc.scalar.activation(not_yet[1][:], before[1][:, :S], ACT.Copy, scale=-0.2, bias=0.2)
+        for b in range(BLOCKS):
+            for d in range(D):
+                add_turned(second_sum[b], weight[d], first=(d == 0), last=False)
+
+        pressure(before[1], first_sum[1], False, "a1")
+        first_decay.append(decay(first_sum[1], "a1", "back1"))
+
+        stays = []
+        for b in range(BLOCKS):
+            own = keep.tile([P, S], F32, name=f"own{b}")
+            nc.vector.scalar_tensor_tensor(own[:], half[b][:], 4.0, not_yet[b][:], ALU.subtract, ALU.mult)
+            nc.vector.tensor_tensor(left[b][:, :S], first_decay[b][:], own[:], ALU.mult)
+            pressure(left[b], second_sum[b], True, f"b{b}")
+            stay = keep.tile([P, S], F32, name=f"stay{b}")
+            nc.vector.scalar_tensor_tensor(stay[:], half[b][:], 4.0, left[b][:, :S], ALU.subtract, ALU.mult)
+            stays.append(stay)
+        for b in range(BLOCKS):
+            back = decay(second_sum[b], f"b{b}", f"y{b}")
+            prod = keep.tile([P, S], F32, name=f"prod{b}")
+            nc.vector.tensor_tensor(prod[:], back[:], stays[b][:], ALU.mult)
+            res = keep.tile([P, S], F32, name=f"res{b}")
+            nc.scalar.activation(res[:], prod[:], ACT.Copy, scale=-0.2, bias=1.0)
+            nc.sync.dma_start(out[b * P : (b + 1) * P, :], res[:])

@@ -1,3 +1,4 @@
+import math
 from contextlib import ExitStack
 
 import concourse.mybir as mybir
@@ -18,6 +19,7 @@ P = 128
 BLOCKS = N // P
 CHUNKS = S // P
 SPARE = 16
+LAST = 128
 FLOPS = 2 * K * N * S
 
 
@@ -30,101 +32,147 @@ def tile_picked_ybassn_two_p_kernel(tc, x_words, x_scales, w1, adopt, infl, offs
         pos_dram = (pos1, pos2, pos3)
         pos = [keep.tile([P, S // 16], U16, name=f"pos{d}") for d in range(D)]
         picks = keep.tile([P, S // 16], U16, name="picks")
-        before = [keep.tile([P, S + SPARE], F32, name=f"before{b}") for b in range(BLOCKS)]
-        left = [keep.tile([P, S + SPARE], F32, name=f"left{b}") for b in range(BLOCKS)]
+        before = [keep.tile([P, S], F32, name=f"before{b}") for b in range(BLOCKS)]
+        not_yet = [keep.tile([P, S + SPARE], F32, name=f"not_yet{b}") for b in range(BLOCKS)]
+        resist = [keep.tile([P, S + SPARE], F32, name=f"resist{b}") for b in range(BLOCKS)]
         weight = [keep.tile([P, S], F32, name=f"weight{d}") for d in range(D)]
         w_raw = keep.tile([P, 4, N], F32, name="w_raw")
         words = keep.tile([P, T], I32, name="words")
         bytes_in = keep.tile([P, T], U8, name="bytes_in")
         ident = keep.tile([P, P], F32, name="ident")
+        rows = keep.tile([P, D, P], F32, name="rows")
 
+        def load_scales(engine, q):
+            engine.dma_start(bytes_in[32 * q : 32 * q + 4, :].bitcast(I32), x_scales[0, 4 * q : 4 * q + 4, :].bitcast(I32))
+
+        nc.gpsimd.memset(bytes_in[:].bitcast(I32), 0)
         make_identity(nc, ident[:])
+        nc.vector.memset(rows[:], 0.0)
         for b in range(BLOCKS):
-            nc.vector.memset(before[b][:, S:], 0.0)
-            nc.vector.memset(left[b][:, S:], 0.0)
-        nc.vector.memset(bytes_in[:].bitcast(I32), 0)
-        for q in range(4):
-            nc.gpsimd.dma_start(bytes_in[32 * q : 32 * q + 4, :].bitcast(I32), x_scales[0, 4 * q : 4 * q + 4, :].bitcast(I32))
-
+            nc.vector.memset(not_yet[b][:, S:], 0.0)
+            nc.vector.memset(resist[b][:, S:], 0.0)
+        nc.gpsimd.dma_start(rows[0:CHUNKS, :, :], infl[:, 0, :].rearrange("d (c j) -> c d j", c=CHUNKS))
         nc.sync.dma_start(pos[0][:], pos_dram[0])
-        nc.sync.dma_start(before[0][:, :S], adopt[0:P, :])
+        nc.sync.dma_start(before[0][:], adopt[0:P, :])
         nc.sync.dma_start(weight[0][:], infl[0])
         for d in range(1, D):
             nc.sync.dma_start(pos[d][:], pos_dram[d])
             nc.sync.dma_start(weight[d][:], infl[d])
+        nc.sync.dma_start(before[1][:], adopt[P : 2 * P, :])
         nc.sync.dma_start(w_raw[:], w1.rearrange("(p j) n -> p j n", j=4))
         nc.sync.dma_start(picks[:], offs)
         nc.sync.dma_start(words[:], x_words[0].rearrange("p n t -> p (n t)").bitcast(I32))
-        nc.sync.dma_start(before[1][:, :S], adopt[P : 2 * P, :])
+        for q in range(4):
+            load_scales(nc.sync, q)
 
-        def add_turned(bank, src, first, last):
-            for c in range(CHUNKS):
-                cols = slice(c * P, (c + 1) * P)
-                nc.tensor.matmul(bank[:, cols], src[:, cols], ident[:], start=first and c == 0, stop=last and c == CHUNKS - 1, is_transpose=True)
+        def add_turned(bank, src, lo, hi, first, last, eye):
+            for c in range(lo, hi, P):
+                nc.tensor.matmul(bank[:, c - lo : c - lo + P], src[:, c : c + P], eye[:],
+                                 start=first and c == lo, stop=last and c == hi - P, is_transpose=True)
 
-        def pressure(window, bank, opened, tag):
-            for d in range(D):
-                term = keep.tile([P, S], F32, name=f"term{tag}{d}")
-                nc.vector.tensor_tensor(term[:], window[:].indirect(pos[d][:]), weight[d][:], ALU.mult)
-                add_turned(bank, term, first=(d == 0 and not opened), last=(d == D - 1))
+        def gather_term(term, window, d, factor, lo, hi):
+            nc.vector.tensor_tensor(term[:, lo:hi], window[:].indirect(pos[d][:, lo // 16 : hi // 16]), factor[:, lo:hi], ALU.mult)
 
-        def decay(bank, tag, bank_tag):
-            turned = keep.tile([P, S], F32, name=f"turned{tag}")
-            nc.scalar.activation(turned[:], bank[:], ACT.Exp, scale=-1.0)
-            back = psum.tile([P, S], F32, name=f"back{tag}", tag=bank_tag)
-            for c in range(CHUNKS):
-                cols = slice(c * P, (c + 1) * P)
-                nc.tensor.transpose(back[:, cols], turned[:, cols], ident[:])
+        def decay(bank, lo, hi, shift, tag, bank_tag):
+            turned = keep.tile([P, hi - lo], F32, name=f"turned{tag}")
+            back = psum.tile([P, hi - lo], F32, name=f"back{tag}", tag=bank_tag)
+            for c in range(lo, hi, P):
+                nc.scalar.activation(turned[:, c - lo : c - lo + P], bank[:, c - lo : c - lo + P], ACT.Exp, scale=2.0, bias=shift[:, c // P : c // P + 1])
+            for c in range(0, hi - lo, P):
+                nc.tensor.transpose(back[:, c : c + P], turned[:, c : c + P], ident[:])
             return back
 
         first_sum = [psum.tile([P, S], F32, name=f"first_sum{b}", tag=f"first{b}") for b in range(BLOCKS)]
-        second_sum = [psum.tile([P, S], F32, name=f"second_sum{b}", tag=f"second{b}") for b in range(BLOCKS)]
+        pieces = [(0, 0, S), (1, 0, S - LAST), (1, S - LAST, S)]
+        second_sum = [psum.tile([P, hi - lo], F32, name=f"second_sum{i}", tag=f"second{i}") for i, (b, lo, hi) in enumerate(pieces)]
+        half = [keep.tile([P, S], F32, name=f"half{b}") for b in range(BLOCKS)]
+        first_terms = [[], []]
 
-        not_yet = [keep.tile([P, S], F32, name=f"not_yet{b}") for b in range(BLOCKS)]
-        nc.scalar.activation(not_yet[0][:], before[0][:, :S], ACT.Copy, scale=-0.2, bias=0.2)
+        def first_term(b, d, term):
+            first_terms[b].append(term)
+            gather_term(term, not_yet[b], d, weight[d], 0, S)
+            add_turned(first_sum[b], term, 0, S, d == 0, d == D - 1, ident)
 
-        pressure(before[0], first_sum[0], False, "a0")
-        first_decay = [decay(first_sum[0], "a0", "back0")]
+        def add_first_terms_again(b):
+            for i, (pb, lo, hi) in enumerate(pieces):
+                if pb == b:
+                    for d in range(D):
+                        add_turned(second_sum[i], first_terms[b][d], lo, hi, d == 0, False, ident)
+
+        def make_resist(b, first_decay):
+            nc.vector.scalar_tensor_tensor(resist[b][:, :S], half[b][:], 4.0, first_decay[:], ALU.add, ALU.mult)
+
+        nc.vector.tensor_scalar(not_yet[0][:, :S], before[0][:], -0.5, 0.5, ALU.mult, ALU.add)
+        for d in range(D):
+            first_term(0, d, keep.tile([P, S], F32, name=f"term_a0{d}")[:])
+
+        nc.scalar.activation(not_yet[1][:, :S], before[1][:], ACT.Copy, scale=-0.5, bias=0.5)
+        first_term(1, 0, keep.tile([P, S], F32, name="term_a10")[:])
+
+        total = psum.tile([P, P], F32, name="total", tag="y1")
+        for d in range(D):
+            add_turned(total, rows[:, d, :], 0, P, d == 0, d == D - 1, ident)
+        shift_first = keep.tile([P, CHUNKS], F32, name="shift_first")
+        nc.scalar.activation(shift_first[:], total[:, 0:CHUNKS], ACT.Copy, scale=-1.0, bias=math.log(0.2))
+        shift_second = keep.tile([P, CHUNKS], F32, name="shift_second")
+        nc.scalar.activation(shift_second[:], total[:, 0:CHUNKS], ACT.Copy, scale=-2.0)
 
         w_grouped = keep.tile([P, N, 4], BF16, name="w_grouped", align_bytes=64)
-        nc.scalar.copy(w_grouped[:], w_raw[:].rearrange("p j n -> p n j"))
+        nc.scalar.copy(w_grouped[:].rearrange("p (c i) j -> p c j i", i=4), w_raw[:].rearrange("p j (c i) -> p c j i", i=4))
         w_codes = keep.tile([P, N], U32, name="w_codes", align_bytes=64)
         w_scales = keep.tile([P, N], U8, name="w_scales", align_bytes=64)
         nc.vector.quantize_mx(w_codes[:].bitcast(FP8X4), w_scales[:], w_grouped[:].rearrange("p n j -> p (n j)"))
         x_codes = keep.tile([P, S], U32, name="x_codes", align_bytes=64)
         x_bytes = keep.tile([P, S], U8, name="x_bytes", align_bytes=64)
-        nc.vector.tensor_copy(x_bytes[:], bytes_in[:].indirect(picks[:]))
         nc.vector.tensor_copy(x_codes[:], words[:].bitcast(U32).indirect(picks[:]))
-        half = []
+        nc.vector.tensor_copy(x_bytes[:], bytes_in[:].indirect(picks[:]))
+        decay0 = decay(first_sum[0], 0, S, shift_first, "a0", "back0")
         for b in range(BLOCKS):
             cols = slice(b * P, (b + 1) * P)
             y = psum.tile([P, S], F32, name=f"y{b}", tag=f"y{b}")
             nc.tensor.matmul_mx(out=y[:], lhsT=w_codes[:, cols].bitcast(FP8X4), lhsT_scale=w_scales[:, cols],
                                 rhs=x_codes[:].bitcast(FP8X4), rhs_scale=x_bytes[:], start=True, stop=True)
-            t = keep.tile([P, S], F32, name=f"half{b}")
-            nc.scalar.activation(t[:], y[:], ACT.Tanh, scale=0.5)
-            half.append(t)
-        nc.scalar.activation(not_yet[1][:], before[1][:, :S], ACT.Copy, scale=-0.2, bias=0.2)
+            nc.scalar.activation(half[b][:], y[:], ACT.Tanh, scale=-0.5)
+        add_first_terms_again(0)
+
+        terms1 = keep.tile([P, 2 * S], F32, name="terms1", tag="bytes_in")
+        first_term(1, 1, terms1[:, :S])
+        first_term(1, 2, terms1[:, S:])
+        make_resist(0, decay0)
+        decay1 = decay(first_sum[1], 0, S, shift_first, "a1", "first0")
+        ident_late = keep.tile([P, P], F32, name="ident_late", tag="shift_first")
+        nc.scalar.copy(ident_late[:], ident[:])
+        add_first_terms_again(1)
+        own = keep.tile([P, BLOCKS * S], F32, name="own", tag="turneda1")
         for b in range(BLOCKS):
+            nc.scalar.activation(own[:, b * S : (b + 1) * S], half[b][:], ACT.Ln, scale=0.2, bias=0.8)
+
+        def second_period(i, bank_tag):
+            b, lo, hi = pieces[i]
+            if b == 1:
+                add_turned(second_sum[i], own[:, S:], lo, hi, False, False, ident)
             for d in range(D):
-                add_turned(second_sum[b], weight[d], first=(d == 0), last=False)
+                if (b, d) == (0, D - 1):
+                    make_resist(1, decay1)
+                term = keep.tile([P, S], F32, name=f"term_b{i}{d}")
+                gather_term(term, resist[b], d, first_terms[b][d], lo, hi)
+                add_turned(second_sum[i], term, lo, hi, False, (b, d) == (1, D - 1), ident_late)
+            if b == 0:
+                add_turned(second_sum[i], own[:, :S], lo, hi, False, True, ident)
+            return decay(second_sum[i], lo, hi, shift_second, f"b{i}", bank_tag)
 
-        pressure(before[1], first_sum[1], False, "a1")
-        first_decay.append(decay(first_sum[1], "a1", "back1"))
+        def finish(i, back, tag):
+            b, lo, hi = pieces[i]
+            prod = keep.tile([P, hi - lo], F32, name=f"prod{i}", tag=tag)
+            nc.vector.tensor_tensor(prod[:], back[:], not_yet[b][:, lo:hi], ALU.mult)
+            res = keep.tile([P, hi - lo], F32, name=f"res{i}")
+            if i == 1:
+                nc.scalar.activation(res[:], prod[:], ACT.Copy, scale=-2.0, bias=1.0)
+            else:
+                nc.vector.tensor_scalar(res[:], prod[:], -2.0, 1.0, ALU.mult, ALU.add)
+            nc.sync.dma_start(out[b * P : (b + 1) * P, lo:hi], res[:])
 
-        stays = []
-        for b in range(BLOCKS):
-            own = keep.tile([P, S], F32, name=f"own{b}")
-            nc.vector.scalar_tensor_tensor(own[:], half[b][:], 4.0, not_yet[b][:], ALU.subtract, ALU.mult)
-            nc.vector.tensor_tensor(left[b][:, :S], first_decay[b][:], own[:], ALU.mult)
-            pressure(left[b], second_sum[b], True, f"b{b}")
-            stay = keep.tile([P, S], F32, name=f"stay{b}")
-            nc.vector.scalar_tensor_tensor(stay[:], half[b][:], 4.0, left[b][:, :S], ALU.subtract, ALU.mult)
-            stays.append(stay)
-        for b in range(BLOCKS):
-            back = decay(second_sum[b], f"b{b}", f"y{b}")
-            prod = keep.tile([P, S], F32, name=f"prod{b}")
-            nc.vector.tensor_tensor(prod[:], back[:], stays[b][:], ALU.mult)
-            res = keep.tile([P, S], F32, name=f"res{b}")
-            nc.scalar.activation(res[:], prod[:], ACT.Copy, scale=-0.2, bias=1.0)
-            nc.sync.dma_start(out[b * P : (b + 1) * P, :], res[:])
+        backs = [second_period(i, tag) for i, tag in enumerate(("y0", "y1", "first1"))]
+        finish(0, backs[0], "bytes_in")
+        finish(1, backs[1], "prod1")
+        finish(2, backs[2], "prod2")

import math
from contextlib import ExitStack

import concourse.mybir as mybir
from concourse.masks import make_identity

F32 = mybir.dt.float32
BF16 = mybir.dt.bfloat16
I32 = mybir.dt.int32
U32 = mybir.dt.uint32
U16 = mybir.dt.uint16
U8 = mybir.dt.uint8
FP8X4 = mybir.dt.float8_e4m3fn_x4
ACT = mybir.ActivationFunctionType
ALU = mybir.AluOpType

K, T, S, N, D = 512, 2048, 512, 256, 3
P = 128
BLOCKS = N // P
CHUNKS = S // P
SPARE = 16
LAST = 128
FLOPS = 2 * K * N * S


def tile_picked_ybassn_two_p_kernel(tc, x_words, x_scales, w1, adopt, infl, offs, pos1, pos2, pos3, out):
    nc = tc.nc
    with ExitStack() as ctx:
        keep = ctx.enter_context(tc.tile_pool(name="keep", bufs=1))
        psum = ctx.enter_context(tc.psum_pool(name="psum", bufs=1))

        pos_dram = (pos1, pos2, pos3)
        pos = [keep.tile([P, S // 16], U16, name=f"pos{d}") for d in range(D)]
        picks = keep.tile([P, S // 16], U16, name="picks")
        before = [keep.tile([P, S], F32, name=f"before{b}") for b in range(BLOCKS)]
        not_yet = [keep.tile([P, S + SPARE], F32, name=f"not_yet{b}") for b in range(BLOCKS)]
        resist = [keep.tile([P, S + SPARE], F32, name=f"resist{b}") for b in range(BLOCKS)]
        weight = [keep.tile([P, S], F32, name=f"weight{d}") for d in range(D)]
        w_raw = keep.tile([P, 4, N], F32, name="w_raw")
        words = keep.tile([P, T], I32, name="words")
        bytes_in = keep.tile([P, T], U8, name="bytes_in")
        ident = keep.tile([P, P], F32, name="ident")
        rows = keep.tile([P, D, P], F32, name="rows")

        def load_scales(engine, q):
            engine.dma_start(bytes_in[32 * q : 32 * q + 4, :].bitcast(I32), x_scales[0, 4 * q : 4 * q + 4, :].bitcast(I32))

        nc.gpsimd.memset(bytes_in[:].bitcast(I32), 0)
        make_identity(nc, ident[:])
        nc.vector.memset(rows[:], 0.0)
        for b in range(BLOCKS):
            nc.vector.memset(not_yet[b][:, S:], 0.0)
            nc.vector.memset(resist[b][:, S:], 0.0)
        nc.gpsimd.dma_start(rows[0:CHUNKS, :, :], infl[:, 0, :].rearrange("d (c j) -> c d j", c=CHUNKS))
        nc.sync.dma_start(pos[0][:], pos_dram[0])
        nc.sync.dma_start(before[0][:], adopt[0:P, :])
        nc.sync.dma_start(weight[0][:], infl[0])
        for d in range(1, D):
            nc.sync.dma_start(pos[d][:], pos_dram[d])
            nc.sync.dma_start(weight[d][:], infl[d])
        nc.sync.dma_start(before[1][:], adopt[P : 2 * P, :])
        nc.sync.dma_start(w_raw[:], w1.rearrange("(p j) n -> p j n", j=4))
        nc.sync.dma_start(picks[:], offs)
        nc.sync.dma_start(words[:], x_words[0].rearrange("p n t -> p (n t)").bitcast(I32))
        for q in range(4):
            load_scales(nc.sync, q)

        def add_turned(bank, src, lo, hi, first, last, eye):
            for c in range(lo, hi, P):
                nc.tensor.matmul(bank[:, c - lo : c - lo + P], src[:, c : c + P], eye[:],
                                 start=first and c == lo, stop=last and c == hi - P, is_transpose=True)

        def gather_term(term, window, d, factor, lo, hi):
            nc.vector.tensor_tensor(term[:, lo:hi], window[:].indirect(pos[d][:, lo // 16 : hi // 16]), factor[:, lo:hi], ALU.mult)

        def decay(bank, lo, hi, shift, tag, bank_tag):
            turned = keep.tile([P, hi - lo], F32, name=f"turned{tag}")
            back = psum.tile([P, hi - lo], F32, name=f"back{tag}", tag=bank_tag)
            for c in range(lo, hi, P):
                nc.scalar.activation(turned[:, c - lo : c - lo + P], bank[:, c - lo : c - lo + P], ACT.Exp, scale=2.0, bias=shift[:, c // P : c // P + 1])
            for c in range(0, hi - lo, P):
                nc.tensor.transpose(back[:, c : c + P], turned[:, c : c + P], ident[:])
            return back

        first_sum = [psum.tile([P, S], F32, name=f"first_sum{b}", tag=f"first{b}") for b in range(BLOCKS)]
        pieces = [(0, 0, S), (1, 0, S - LAST), (1, S - LAST, S)]
        second_sum = [psum.tile([P, hi - lo], F32, name=f"second_sum{i}", tag=f"second{i}") for i, (b, lo, hi) in enumerate(pieces)]
        half = [keep.tile([P, S], F32, name=f"half{b}") for b in range(BLOCKS)]
        first_terms = [[], []]

        def first_term(b, d, term):
            first_terms[b].append(term)
            gather_term(term, not_yet[b], d, weight[d], 0, S)
            add_turned(first_sum[b], term, 0, S, d == 0, d == D - 1, ident)

        def add_first_terms_again(b):
            for i, (pb, lo, hi) in enumerate(pieces):
                if pb == b:
                    for d in range(D):
                        add_turned(second_sum[i], first_terms[b][d], lo, hi, d == 0, False, ident)

        def make_resist(b, first_decay):
            nc.vector.scalar_tensor_tensor(resist[b][:, :S], half[b][:], 4.0, first_decay[:], ALU.add, ALU.mult)

        nc.vector.tensor_scalar(not_yet[0][:, :S], before[0][:], -0.5, 0.5, ALU.mult, ALU.add)
        for d in range(D):
            first_term(0, d, keep.tile([P, S], F32, name=f"term_a0{d}")[:])

        nc.scalar.activation(not_yet[1][:, :S], before[1][:], ACT.Copy, scale=-0.5, bias=0.5)
        first_term(1, 0, keep.tile([P, S], F32, name="term_a10")[:])

        total = psum.tile([P, P], F32, name="total", tag="y1")
        for d in range(D):
            add_turned(total, rows[:, d, :], 0, P, d == 0, d == D - 1, ident)
        shift_first = keep.tile([P, CHUNKS], F32, name="shift_first")
        nc.scalar.activation(shift_first[:], total[:, 0:CHUNKS], ACT.Copy, scale=-1.0, bias=math.log(0.2))
        shift_second = keep.tile([P, CHUNKS], F32, name="shift_second")
        nc.scalar.activation(shift_second[:], total[:, 0:CHUNKS], ACT.Copy, scale=-2.0)

        w_grouped = keep.tile([P, N, 4], BF16, name="w_grouped", align_bytes=64)
        nc.scalar.copy(w_grouped[:].rearrange("p (c i) j -> p c j i", i=4), w_raw[:].rearrange("p j (c i) -> p c j i", i=4))
        w_codes = keep.tile([P, N], U32, name="w_codes", align_bytes=64)
        w_scales = keep.tile([P, N], U8, name="w_scales", align_bytes=64)
        nc.vector.quantize_mx(w_codes[:].bitcast(FP8X4), w_scales[:], w_grouped[:].rearrange("p n j -> p (n j)"))
        x_codes = keep.tile([P, S], U32, name="x_codes", align_bytes=64)
        x_bytes = keep.tile([P, S], U8, name="x_bytes", align_bytes=64)
        nc.vector.tensor_copy(x_codes[:], words[:].bitcast(U32).indirect(picks[:]))
        nc.vector.tensor_copy(x_bytes[:], bytes_in[:].indirect(picks[:]))
        decay0 = decay(first_sum[0], 0, S, shift_first, "a0", "back0")
        for b in range(BLOCKS):
            cols = slice(b * P, (b + 1) * P)
            y = psum.tile([P, S], F32, name=f"y{b}", tag=f"y{b}")
            nc.tensor.matmul_mx(out=y[:], lhsT=w_codes[:, cols].bitcast(FP8X4), lhsT_scale=w_scales[:, cols],
                                rhs=x_codes[:].bitcast(FP8X4), rhs_scale=x_bytes[:], start=True, stop=True)
            nc.scalar.activation(half[b][:], y[:], ACT.Tanh, scale=-0.5)
        add_first_terms_again(0)

        terms1 = keep.tile([P, 2 * S], F32, name="terms1", tag="bytes_in")
        first_term(1, 1, terms1[:, :S])
        first_term(1, 2, terms1[:, S:])
        make_resist(0, decay0)
        decay1 = decay(first_sum[1], 0, S, shift_first, "a1", "first0")
        ident_late = keep.tile([P, P], F32, name="ident_late", tag="shift_first")
        nc.scalar.copy(ident_late[:], ident[:])
        add_first_terms_again(1)
        own = keep.tile([P, BLOCKS * S], F32, name="own", tag="turneda1")
        for b in range(BLOCKS):
            nc.scalar.activation(own[:, b * S : (b + 1) * S], half[b][:], ACT.Ln, scale=0.2, bias=0.8)

        def second_period(i, bank_tag):
            b, lo, hi = pieces[i]
            if b == 1:
                add_turned(second_sum[i], own[:, S:], lo, hi, False, False, ident)
            for d in range(D):
                if (b, d) == (0, D - 1):
                    make_resist(1, decay1)
                term = keep.tile([P, S], F32, name=f"term_b{i}{d}")
                gather_term(term, resist[b], d, first_terms[b][d], lo, hi)
                add_turned(second_sum[i], term, lo, hi, False, (b, d) == (1, D - 1), ident_late)
            if b == 0:
                add_turned(second_sum[i], own[:, :S], lo, hi, False, True, ident)
            return decay(second_sum[i], lo, hi, shift_second, f"b{i}", bank_tag)

        def finish(i, back, tag):
            b, lo, hi = pieces[i]
            prod = keep.tile([P, hi - lo], F32, name=f"prod{i}", tag=tag)
            nc.vector.tensor_tensor(prod[:], back[:], not_yet[b][:, lo:hi], ALU.mult)
            res = keep.tile([P, hi - lo], F32, name=f"res{i}")
            if i == 1:
                nc.scalar.activation(res[:], prod[:], ACT.Copy, scale=-2.0, bias=1.0)
            else:
                nc.vector.tensor_scalar(res[:], prod[:], -2.0, 1.0, ALU.mult, ALU.add)
            nc.sync.dma_start(out[b * P : (b + 1) * P, lo:hi], res[:])

        backs = [second_period(i, tag) for i, tag in enumerate(("y0", "y1", "first1"))]
        finish(0, backs[0], "bytes_in")
        finish(1, backs[1], "prod1")
        finish(2, backs[2], "prod2")
